import numpy as np
import ml_dtypes


def mxq(x, axis, fmt="e4m3"):
    dtype, down = {"e4m3": (ml_dtypes.float8_e4m3fn, 7), "e5m2": (ml_dtypes.float8_e5m2, 14)}[fmt]
    v = np.moveaxis(np.asarray(x, np.float32).astype(ml_dtypes.bfloat16).astype(np.float64), axis, -1)
    blocks = v.reshape(v.shape[:-1] + (-1, 32))
    amax = np.abs(blocks).max(-1, keepdims=True)
    byte = np.maximum(np.where(amax > 0, np.frexp(amax)[1] - 1 + 127, 0) - down, 1)
    scale = np.exp2(byte - 127.0)
    codes = (blocks / scale).astype(np.float32).astype(dtype).astype(np.float64)
    return np.moveaxis((codes * scale).reshape(v.shape), -1, axis)


WIDE = False


def mx_kscale(k):
    if not WIDE:
        return np.ones(k)
    levels = np.array([10, -10, 5, -5, 0])
    if k % 512:
        return np.exp2(np.random.permutation(np.resize(levels, k // 32))).repeat(32)
    a = np.empty((k // 512, 16))
    for p in range(k // 512):
        a[p, :8] = np.random.permutation(np.resize(levels, 8))
        for g in range(8):
            far = levels[np.abs(levels - a[p, g]) >= 10]
            a[p, g + 8] = far[np.random.randint(len(far))]
    return np.exp2(a.ravel()).repeat(32)


def f64(x):
    return np.asarray(x).astype(np.float64)


def striped(idx):
    return np.tile(idx.reshape(-1, 16).T, (8, 1)).astype(np.uint16)


def unstriped(offs):
    return offs[:16].T.reshape(-1).astype(np.int64)


def silu(v):
    return v / (1.0 + np.exp(-np.maximum(v, -700.0)))


K, T, D, S, V, N = 1536, 2048, 4, 768, 192, 128


def setup_inputs():
    n = np.random.standard_normal
    s = mx_kscale(K)[:, None]
    return {
        "xT": (n((K, T)) * s).astype(np.float32),
        "w": (n((K, N)) / np.sqrt(K) / s).astype(np.float32),
        "b": (0.3 * n((N, 1))).astype(np.float32),
        "offs": striped(np.random.permutation(T)[:S]),
    }


def reference(xT, w, b, offs):
    idx = unstriped(offs)
    xq = mxq(f64(xT)[:, idx], 0, "e4m3")
    y = mxq(f64(w), 0, "e4m3").T @ xq
    y = silu(y + f64(b))
    return y.reshape(N, V, D).max(axis=2)

@@ -1,0 +1,156 @@
+from contextlib import ExitStack
+
+import concourse.mybir as mybir
+
+F32 = mybir.dt.float32
+BF16 = mybir.dt.bfloat16
+U32 = mybir.dt.uint32
+U16 = mybir.dt.uint16
+U8 = mybir.dt.uint8
+FP8X4 = mybir.dt.float8_e4m3fn_x4
+COPY = mybir.ActivationFunctionType.Copy
+SILU = mybir.ActivationFunctionType.Silu
+
+P = 128
+K, T, S, D, N = 1536, 2048, 768, 4, 128
+PASSES = K // 512
+PIECE = 256
+PIECES = S // PIECE
+FLOPS = 2 * N * S * K
+
+V_COLS = 768
+LAST_CHUNKS = [(0, 1024, 384), (1024, 512, 192), (1536, 512, 352)]
+
+
+def tile_picked_pool_lin_silu_sub_e_kernel(tc, xT, w, b, offs, out):
+    nc = tc.nc
+    with ExitStack() as ctx:
+        keep = ctx.enter_context(tc.tile_pool(name="keep", bufs=1))
+        psum = ctx.enter_context(tc.psum_pool(name="psum", bufs=1))
+
+        offsets = keep.tile([P, S // 16], U16, name="offsets")
+        nc.sync.dma_start(offsets[:], offs)
+        bias = keep.tile([P, 1], F32, name="bias")
+        nc.scalar.dma_start(bias[:], b)
+        warm = keep.tile([P, 1], F32, name="warm")
+        nc.vector.memset(warm[:], 0.0)
+        warm_out = keep.tile([P, 1], F32, name="warm_out")
+        nc.scalar.activation(warm_out[:], warm[:], SILU)
+
+        chunks = {}
+        for a in range(PASSES):
+            rows = xT[512 * a : 512 * (a + 1), :].rearrange("(p j) t -> p j t", j=4)
+            for u in range(2):
+                last = a == PASSES - 1 and u == 1
+                spans = LAST_CHUNKS if last else [(0, T, V_COLS)]
+                got = []
+                for c0, width, share in spans:
+                    raw = keep.tile([P, 2, width], F32, name=f"raw{a}_{u}_{c0}")
+                    nc.sync.dma_start(raw[:], rows[:, 2 * u : 2 * u + 2, c0 : c0 + width])
+                    got.append((c0, width, share, raw))
+                chunks[a, u] = got
+        w_raw = []
+        for a in range(PASSES):
+            raw = keep.tile([P, 4, N], F32, name=f"w_raw{a}")
+            nc.sync.dma_start(raw[:], w[512 * a : 512 * (a + 1), :].rearrange("(p j) n -> p j n", j=4))
+            w_raw.append(raw)
+
+        grouped = []
+        codes = []
+        scales = []
+        for a in range(PASSES):
+            grouped.append(keep.tile([P, 4 * S], BF16, name=f"grouped{a}", align_bytes=64))
+            codes.append(keep.tile([P, S], U32, name=f"codes{a}", align_bytes=64))
+            scales.append(keep.tile([P, S], U8, name=f"scales{a}", align_bytes=64))
+
+        def cast(a, u, window):
+            pairs = window[:].rearrange("p (t j) -> p t j", j=2)
+            for c0, width, share, raw in chunks[a, u]:
+                cut = width - share
+                src = raw[:].rearrange("p j t -> p t j")
+                nc.scalar.activation(pairs[:, c0 : c0 + cut, :], src[:, :cut, :], COPY)
+                nc.vector.tensor_copy(pairs[:, c0 + cut : c0 + width, :], src[:, cut:, :])
+
+        def gather(a, u, window, n0, n):
+            words = grouped[a][:].bitcast(U32).rearrange("p (n u) -> p n u", u=2)
+            nc.vector.tensor_copy(
+                words[:, n0 : n0 + n, u],
+                window[:].bitcast(U32).indirect(offsets[:, n0 // 16 : (n0 + n) // 16]),
+            )
+
+        def quantize(a, n0, n):
+            nc.vector.quantize_mx(
+                out=codes[a][:, n0 : n0 + n].bitcast(FP8X4),
+                scales=scales[a][:, n0 : n0 + n],
+                in_=grouped[a][:, 4 * n0 : 4 * (n0 + n)],
+            )
+
+        for a in range(PASSES):
+            for u in range(2):
+                window = keep.tile([P, 2 * T], BF16, name=f"pairs{a}_{u}")
+                cast(a, u, window)
+                if a > 0 and u == 0:
+                    quantize(a - 1, 0, 512)
+                    quantize(a - 1, 512, 256)
+                if a < PASSES - 1 or u == 0:
+                    gather(a, u, window, 0, S)
+
+        w_codes = keep.tile([P, PASSES, N], U32, name="w_codes", align_bytes=64)
+        w_scales = keep.tile([P, PASSES, N], U8, name="w_scales", align_bytes=64)
+        w_grouped = keep.tile([P, PASSES, 4 * N], BF16, name="w_grouped", align_bytes=64)
+        for a in range(PASSES):
+            nc.scalar.activation(
+                w_grouped[:, a, :].rearrange("p (n j) -> p n j", j=4), w_raw[a][:].rearrange("p j n -> p n j"), COPY
+            )
+
+        def quantize_w(a):
+            nc.vector.quantize_mx(
+                out=w_codes[:, a, :].bitcast(FP8X4), scales=w_scales[:, a, :], in_=w_grouped[:, a, :]
+            )
+
+        banks = [psum.tile([P, PIECE], F32, name=f"bank{i}") for i in range(PIECES)]
+
+        def multiply(a, i):
+            cols = slice(PIECE * i, PIECE * (i + 1))
+            nc.tensor.matmul_mx(
+                out=banks[i][:],
+                lhsT=w_codes[:, a, :].bitcast(FP8X4),
+                lhsT_scale=w_scales[:, a, :],
+                rhs=codes[a][:, cols].bitcast(FP8X4),
+                rhs_scale=scales[a][:, cols],
+                start=(a == 0),
+                stop=(a == PASSES - 1),
+            )
+
+        result = keep.tile([P, S // D], F32, name="result")
+
+        def finish(i):
+            y = keep.tile([P, PIECE], F32, name=f"y{i}")
+            nc.scalar.activation(y[:], banks[i][:], SILU, bias=bias[:])
+            nc.vector.tensor_reduce(
+                result[:, PIECE // D * i : PIECE // D * (i + 1)],
+                y[:].rearrange("p (v d) -> p v d", d=D),
+                mybir.AxisListType.X,
+                mybir.AluOpType.max,
+            )
+
+        last = PASSES - 1
+        gather(last, 1, window, 0, PIECE)
+        gather(last, 1, window, PIECE, PIECE)
+        quantize_w(0)
+        for i in range(PIECES):
+            multiply(0, i)
+        quantize(last, 0, PIECE)
+        gather(last, 1, window, 2 * PIECE, PIECE)
+        quantize_w(1)
+        for i in range(PIECES):
+            multiply(1, i)
+        quantize_w(2)
+        multiply(2, 0)
+        quantize(last, PIECE, PIECE)
+        multiply(2, 1)
+        quantize(last, 2 * PIECE, PIECE)
+        multiply(2, 2)
+        for i in range(PIECES):
+            finish(i)
+        nc.sync.dma_start(out, result[:])

@@ -15,11 +15,12 @@ P = 128
 K, T, S, D, N = 1536, 2048, 768, 4, 128
 PASSES = K // 512
 PIECE = 256
-PIECES = S // PIECE
+CUTS = [(0, 256), (256, 256), (512, 128), (640, 128)]
 FLOPS = 2 * N * S * K
 
-V_COLS = 768
-LAST_CHUNKS = [(0, 1024, 384), (1024, 512, 192), (1536, 512, 352)]
+WHOLE = [(0, T, 384)]
+HALVES = [(0, 1024, 192), (1024, 1024, 192)]
+LAST_CHUNKS = [(0, 1024, 256), (1024, 512, 128), (1536, 512, 352)]
 
 
 def tile_picked_pool_lin_silu_sub_e_kernel(tc, xT, w, b, offs, out):
@@ -41,8 +42,7 @@ def tile_picked_pool_lin_silu_sub_e_kernel(tc, xT, w, b, offs, out):
         for a in range(PASSES):
             rows = xT[512 * a : 512 * (a + 1), :].rearrange("(p j) t -> p j t", j=4)
             for u in range(2):
-                last = a == PASSES - 1 and u == 1
-                spans = LAST_CHUNKS if last else [(0, T, V_COLS)]
+                spans = WHOLE if a < PASSES - 1 else HALVES if u == 0 else LAST_CHUNKS
                 got = []
                 for c0, width, share in spans:
                     raw = keep.tile([P, 2, width], F32, name=f"raw{a}_{u}_{c0}")
@@ -108,10 +108,11 @@ def tile_picked_pool_lin_silu_sub_e_kernel(tc, xT, w, b, offs, out):
                 out=w_codes[:, a, :].bitcast(FP8X4), scales=w_scales[:, a, :], in_=w_grouped[:, a, :]
             )
 
-        banks = [psum.tile([P, PIECE], F32, name=f"bank{i}") for i in range(PIECES)]
+        banks = [psum.tile([P, n], F32, name=f"bank{i}") for i, (n0, n) in enumerate(CUTS)]
 
         def multiply(a, i):
-            cols = slice(PIECE * i, PIECE * (i + 1))
+            n0, n = CUTS[i]
+            cols = slice(n0, n0 + n)
             nc.tensor.matmul_mx(
                 out=banks[i][:],
                 lhsT=w_codes[:, a, :].bitcast(FP8X4),
@@ -125,10 +126,12 @@ def tile_picked_pool_lin_silu_sub_e_kernel(tc, xT, w, b, offs, out):
         result = keep.tile([P, S // D], F32, name="result")
 
         def finish(i):
-            y = keep.tile([P, PIECE], F32, name=f"y{i}")
+            n0, n = CUTS[i]
+            y = keep.tile([P, n], F32, name=f"y{i}")
             nc.scalar.activation(y[:], banks[i][:], SILU, bias=bias[:])
+            v0 = n0 // D
             nc.vector.tensor_reduce(
-                result[:, PIECE // D * i : PIECE // D * (i + 1)],
+                result[:, v0 : v0 + n // D],
                 y[:].rearrange("p (v d) -> p v d", d=D),
                 mybir.AxisListType.X,
                 mybir.AluOpType.max,
@@ -138,19 +141,23 @@ def tile_picked_pool_lin_silu_sub_e_kernel(tc, xT, w, b, offs, out):
         gather(last, 1, window, 0, PIECE)
         gather(last, 1, window, PIECE, PIECE)
         quantize_w(0)
-        for i in range(PIECES):
+        for i in range(len(CUTS)):
             multiply(0, i)
         quantize(last, 0, PIECE)
         gather(last, 1, window, 2 * PIECE, PIECE)
         quantize_w(1)
-        for i in range(PIECES):
+        for i in range(len(CUTS)):
             multiply(1, i)
         quantize_w(2)
         multiply(2, 0)
         quantize(last, PIECE, PIECE)
         multiply(2, 1)
-        quantize(last, 2 * PIECE, PIECE)
+        quantize(last, 512, 128)
         multiply(2, 2)
-        for i in range(PIECES):
-            finish(i)
+        finish(0)
+        quantize(last, 640, 128)
+        multiply(2, 3)
+        finish(1)
+        finish(2)
+        finish(3)
         nc.sync.dma_start(out, result[:])

@@ -1,6 +1,7 @@
 from contextlib import ExitStack
 
 import concourse.mybir as mybir
+from concourse.masks import make_identity
 
 F32 = mybir.dt.float32
 BF16 = mybir.dt.bfloat16
@@ -16,6 +17,7 @@ K, T, S, D, N = 1536, 2048, 768, 4, 128
 PASSES = K // 512
 PIECE = 256
 CUTS = [(0, 256), (256, 256), (512, 128), (640, 128)]
+WARM = (24, 16, 0)
 FLOPS = 2 * N * S * K
 
 WHOLE = [(0, T, 384)]
@@ -30,9 +32,9 @@ def tile_picked_pool_lin_silu_sub_e_kernel(tc, xT, w, b, offs, out):
         psum = ctx.enter_context(tc.psum_pool(name="psum", bufs=1))
 
         offsets = keep.tile([P, S // 16], U16, name="offsets")
-        nc.sync.dma_start(offsets[:], offs)
         bias = keep.tile([P, 1], F32, name="bias")
-        nc.scalar.dma_start(bias[:], b)
+        identity = keep.tile([P, P], BF16, name="identity")
+        make_identity(nc, identity[:])
         warm = keep.tile([P, 1], F32, name="warm")
         nc.vector.memset(warm[:], 0.0)
         warm_out = keep.tile([P, 1], F32, name="warm_out")
@@ -49,6 +51,9 @@ def tile_picked_pool_lin_silu_sub_e_kernel(tc, xT, w, b, offs, out):
                     nc.sync.dma_start(raw[:], rows[:, 2 * u : 2 * u + 2, c0 : c0 + width])
                     got.append((c0, width, share, raw))
                 chunks[a, u] = got
+                if (a, u) == (0, 0):
+                    nc.sync.dma_start(offsets[:], offs)
+                    nc.sync.dma_start(bias[:], b)
         w_raw = []
         for a in range(PASSES):
             raw = keep.tile([P, 4, N], F32, name=f"w_raw{a}")
@@ -63,13 +68,18 @@ def tile_picked_pool_lin_silu_sub_e_kernel(tc, xT, w, b, offs, out):
             codes.append(keep.tile([P, S], U32, name=f"codes{a}", align_bytes=64))
             scales.append(keep.tile([P, S], U8, name=f"scales{a}", align_bytes=64))
 
+        spare = psum.tile([P, P], BF16, name="spare")
+
         def cast(a, u, window):
             pairs = window[:].rearrange("p (t j) -> p t j", j=2)
-            for c0, width, share, raw in chunks[a, u]:
+            for at, (c0, width, share, raw) in enumerate(chunks[a, u]):
                 cut = width - share
                 src = raw[:].rearrange("p j t -> p t j")
                 nc.scalar.activation(pairs[:, c0 : c0 + cut, :], src[:, :cut, :], COPY)
                 nc.vector.tensor_copy(pairs[:, c0 + cut : c0 + width, :], src[:, cut:, :])
+                if (a, u) == (PASSES - 1, 1):
+                    for i in range(WARM[at]):
+                        nc.tensor.transpose(spare[:], window[:, 2 * c0 + P * (i % 8) : 2 * c0 + P * (i % 8 + 1)], identity[:])
 
         def gather(a, u, window, n0, n):
             words = grouped[a][:].bitcast(U32).rearrange("p (n u) -> p n u", u=2)

from contextlib import ExitStack

import concourse.mybir as mybir
from concourse.masks import make_identity

F32 = mybir.dt.float32
BF16 = mybir.dt.bfloat16
U32 = mybir.dt.uint32
U16 = mybir.dt.uint16
U8 = mybir.dt.uint8
FP8X4 = mybir.dt.float8_e4m3fn_x4
COPY = mybir.ActivationFunctionType.Copy
SILU = mybir.ActivationFunctionType.Silu

P = 128
K, T, S, D, N = 1536, 2048, 768, 4, 128
PASSES = K // 512
PIECE = 256
CUTS = [(0, 256), (256, 256), (512, 128), (640, 128)]
WARM = (24, 16, 0)
FLOPS = 2 * N * S * K

WHOLE = [(0, T, 384)]
HALVES = [(0, 1024, 192), (1024, 1024, 192)]
LAST_CHUNKS = [(0, 1024, 256), (1024, 512, 128), (1536, 512, 352)]


def tile_picked_pool_lin_silu_sub_e_kernel(tc, xT, w, b, offs, out):
    nc = tc.nc
    with ExitStack() as ctx:
        keep = ctx.enter_context(tc.tile_pool(name="keep", bufs=1))
        psum = ctx.enter_context(tc.psum_pool(name="psum", bufs=1))

        offsets = keep.tile([P, S // 16], U16, name="offsets")
        bias = keep.tile([P, 1], F32, name="bias")
        identity = keep.tile([P, P], BF16, name="identity")
        make_identity(nc, identity[:])
        warm = keep.tile([P, 1], F32, name="warm")
        nc.vector.memset(warm[:], 0.0)
        warm_out = keep.tile([P, 1], F32, name="warm_out")
        nc.scalar.activation(warm_out[:], warm[:], SILU)

        chunks = {}
        for a in range(PASSES):
            rows = xT[512 * a : 512 * (a + 1), :].rearrange("(p j) t -> p j t", j=4)
            for u in range(2):
                spans = WHOLE if a < PASSES - 1 else HALVES if u == 0 else LAST_CHUNKS
                got = []
                for c0, width, share in spans:
                    raw = keep.tile([P, 2, width], F32, name=f"raw{a}_{u}_{c0}")
                    nc.sync.dma_start(raw[:], rows[:, 2 * u : 2 * u + 2, c0 : c0 + width])
                    got.append((c0, width, share, raw))
                chunks[a, u] = got
                if (a, u) == (0, 0):
                    nc.sync.dma_start(offsets[:], offs)
                    nc.sync.dma_start(bias[:], b)
        w_raw = []
        for a in range(PASSES):
            raw = keep.tile([P, 4, N], F32, name=f"w_raw{a}")
            nc.sync.dma_start(raw[:], w[512 * a : 512 * (a + 1), :].rearrange("(p j) n -> p j n", j=4))
            w_raw.append(raw)

        grouped = []
        codes = []
        scales = []
        for a in range(PASSES):
            grouped.append(keep.tile([P, 4 * S], BF16, name=f"grouped{a}", align_bytes=64))
            codes.append(keep.tile([P, S], U32, name=f"codes{a}", align_bytes=64))
            scales.append(keep.tile([P, S], U8, name=f"scales{a}", align_bytes=64))

        spare = psum.tile([P, P], BF16, name="spare")

        def cast(a, u, window):
            pairs = window[:].rearrange("p (t j) -> p t j", j=2)
            for at, (c0, width, share, raw) in enumerate(chunks[a, u]):
                cut = width - share
                src = raw[:].rearrange("p j t -> p t j")
                nc.scalar.activation(pairs[:, c0 : c0 + cut, :], src[:, :cut, :], COPY)
                nc.vector.tensor_copy(pairs[:, c0 + cut : c0 + width, :], src[:, cut:, :])
                if (a, u) == (PASSES - 1, 1):
                    for i in range(WARM[at]):
                        nc.tensor.transpose(spare[:], window[:, 2 * c0 + P * (i % 8) : 2 * c0 + P * (i % 8 + 1)], identity[:])

        def gather(a, u, window, n0, n):
            words = grouped[a][:].bitcast(U32).rearrange("p (n u) -> p n u", u=2)
            nc.vector.tensor_copy(
                words[:, n0 : n0 + n, u],
                window[:].bitcast(U32).indirect(offsets[:, n0 // 16 : (n0 + n) // 16]),
            )

        def quantize(a, n0, n):
            nc.vector.quantize_mx(
                out=codes[a][:, n0 : n0 + n].bitcast(FP8X4),
                scales=scales[a][:, n0 : n0 + n],
                in_=grouped[a][:, 4 * n0 : 4 * (n0 + n)],
            )

        for a in range(PASSES):
            for u in range(2):
                window = keep.tile([P, 2 * T], BF16, name=f"pairs{a}_{u}")
                cast(a, u, window)
                if a > 0 and u == 0:
                    quantize(a - 1, 0, 512)
                    quantize(a - 1, 512, 256)
                if a < PASSES - 1 or u == 0:
                    gather(a, u, window, 0, S)

        w_codes = keep.tile([P, PASSES, N], U32, name="w_codes", align_bytes=64)
        w_scales = keep.tile([P, PASSES, N], U8, name="w_scales", align_bytes=64)
        w_grouped = keep.tile([P, PASSES, 4 * N], BF16, name="w_grouped", align_bytes=64)
        for a in range(PASSES):
            nc.scalar.activation(
                w_grouped[:, a, :].rearrange("p (n j) -> p n j", j=4), w_raw[a][:].rearrange("p j n -> p n j"), COPY
            )

        def quantize_w(a):
            nc.vector.quantize_mx(
                out=w_codes[:, a, :].bitcast(FP8X4), scales=w_scales[:, a, :], in_=w_grouped[:, a, :]
            )

        banks = [psum.tile([P, n], F32, name=f"bank{i}") for i, (n0, n) in enumerate(CUTS)]

        def multiply(a, i):
            n0, n = CUTS[i]
            cols = slice(n0, n0 + n)
            nc.tensor.matmul_mx(
                out=banks[i][:],
                lhsT=w_codes[:, a, :].bitcast(FP8X4),
                lhsT_scale=w_scales[:, a, :],
                rhs=codes[a][:, cols].bitcast(FP8X4),
                rhs_scale=scales[a][:, cols],
                start=(a == 0),
                stop=(a == PASSES - 1),
            )

        result = keep.tile([P, S // D], F32, name="result")

        def finish(i):
            n0, n = CUTS[i]
            y = keep.tile([P, n], F32, name=f"y{i}")
            nc.scalar.activation(y[:], banks[i][:], SILU, bias=bias[:])
            v0 = n0 // D
            nc.vector.tensor_reduce(
                result[:, v0 : v0 + n // D],
                y[:].rearrange("p (v d) -> p v d", d=D),
                mybir.AxisListType.X,
                mybir.AluOpType.max,
            )

        last = PASSES - 1
        gather(last, 1, window, 0, PIECE)
        gather(last, 1, window, PIECE, PIECE)
        quantize_w(0)
        for i in range(len(CUTS)):
            multiply(0, i)
        quantize(last, 0, PIECE)
        gather(last, 1, window, 2 * PIECE, PIECE)
        quantize_w(1)
        for i in range(len(CUTS)):
            multiply(1, i)
        quantize_w(2)
        multiply(2, 0)
        quantize(last, PIECE, PIECE)
        multiply(2, 1)
        quantize(last, 512, 128)
        multiply(2, 2)
        finish(0)
        quantize(last, 640, 128)
        multiply(2, 3)
        finish(1)
        finish(2)
        finish(3)
        nc.sync.dma_start(out, result[:])
